import numpy as np
import ml_dtypes


def mxq(x, axis, fmt="e4m3"):
    dtype, down = {"e4m3": (ml_dtypes.float8_e4m3fn, 7), "e5m2": (ml_dtypes.float8_e5m2, 14)}[fmt]
    v = np.moveaxis(np.asarray(x, np.float32).astype(ml_dtypes.bfloat16).astype(np.float64), axis, -1)
    blocks = v.reshape(v.shape[:-1] + (-1, 32))
    amax = np.abs(blocks).max(-1, keepdims=True)
    byte = np.maximum(np.where(amax > 0, np.frexp(amax)[1] - 1 + 127, 0) - down, 1)
    scale = np.exp2(byte - 127.0)
    codes = (blocks / scale).astype(np.float32).astype(dtype).astype(np.float64)
    return np.moveaxis((codes * scale).reshape(v.shape), -1, axis)


WIDE = False


def mx_kscale(k):
    if not WIDE:
        return np.ones(k)
    levels = np.array([10, -10, 5, -5, 0])
    if k % 512:
        return np.exp2(np.random.permutation(np.resize(levels, k // 32))).repeat(32)
    a = np.empty((k // 512, 16))
    for p in range(k // 512):
        a[p, :8] = np.random.permutation(np.resize(levels, 8))
        for g in range(8):
            far = levels[np.abs(levels - a[p, g]) >= 10]
            a[p, g + 8] = far[np.random.randint(len(far))]
    return np.exp2(a.ravel()).repeat(32)


def f64(x):
    return np.asarray(x).astype(np.float64)


def striped(idx):
    return np.tile(idx.reshape(-1, 16).T, (8, 1)).astype(np.uint16)


def unstriped(offs):
    return offs[:16].T.reshape(-1).astype(np.int64)


E2M1 = np.array([0.0, 0.5, 1.0, 1.5, 2.0, 3.0, 4.0, 6.0, -0.0, -0.5, -1.0, -1.5, -2.0, -3.0, -4.0, -6.0])


def pack_fp4(w):
    k, n = w.shape
    w = f64(np.asarray(w, np.float32).astype(ml_dtypes.bfloat16)).reshape(k // 32, 32, n)
    amax = np.abs(w).max(1)
    mant, ex = np.frexp(amax / 6.0)
    byte = np.clip(np.where(amax > 0, np.where(mant > 0.5, ex, ex - 1) + 127, 1), 1, 254)
    scaled = (w * np.exp2(127.0 - byte)[:, None, :]).reshape(k, n).astype(np.float32)
    c = np.ascontiguousarray(scaled.reshape(k // 512, 128, 4, n).transpose(0, 1, 3, 2)).astype(ml_dtypes.float4_e2m1fn).view(np.uint8) & 0xF
    words = (c[..., 0::2] | (c[..., 1::2] << 4)).reshape(k // 512, 128, 2 * n)
    return np.ascontiguousarray(words), np.ascontiguousarray(byte.astype(np.uint8).reshape(k // 512, 16, n))


def unpack_fp4(words, scales):
    g, _, n = scales.shape
    words = np.ascontiguousarray(words).reshape(g, 128, n, 2)
    nib = np.empty((g, 128, n, 4), np.uint8)
    nib[..., 0::2] = words & 0xF
    nib[..., 1::2] = words >> 4
    vals = E2M1[nib] * np.repeat(np.exp2(scales.astype(np.float64) - 127.0), 8, axis=1)[..., None]
    return vals.transpose(0, 1, 3, 2).reshape(g * 512, n)


def relu(v):
    return np.maximum(v, 0.0)


K, T, S, V, H, N, J = 512, 2048, 1024, 512, 512, 256, 512


def setup_inputs():
    n = np.random.standard_normal
    s = mx_kscale(K)[:, None]
    u = mx_kscale(H)
    r = mx_kscale(J)[:, None]
    packed_w4 = pack_fp4(n((H, N)) / np.sqrt(H) / u[:, None])
    return {
        "xT": (n((K, T)) * s).astype(np.float32),
        "eT": (n((J, V)) * r).astype(np.float32),
        "w1": (n((K, H)) / np.sqrt(3 * K) / s * u).astype(np.float32),
        "w2": (n((K, H)) / np.sqrt(3 * K) / s * u).astype(np.float32),
        "w3": (n((J, H)) / np.sqrt(3 * J) / r * u).astype(np.float32),
        "w4_words": packed_w4[0],
        "w4_scales": packed_w4[1],
        "offs": striped(np.random.permutation(T)[:S]),
    }


def reference(xT, eT, w1, w2, w3, w4_words, w4_scales, offs):
    xq = mxq(f64(xT)[:, unstriped(offs)], 0, "e4m3")
    h = relu(mxq(f64(w1), 0, "e4m3").T @ xq[:, :V] + mxq(f64(w2), 0, "e4m3").T @ xq[:, V:2 * V] + mxq(f64(w3), 0, "e4m3").T @ mxq(f64(eT), 0, "e4m3"))
    return unpack_fp4(w4_words, w4_scales).T @ mxq(h, 0, "e4m3")

@@ -1,0 +1,178 @@
+from contextlib import ExitStack
+
+import concourse.mybir as mybir
+
+K, T, S, V, H, N = 512, 2048, 1024, 512, 512, 256
+FLOPS = 2 * (3 * K * H * V + H * N * V)
+
+F32 = mybir.dt.float32
+BF16 = mybir.dt.bfloat16
+I32 = mybir.dt.int32
+U32 = mybir.dt.uint32
+U16 = mybir.dt.uint16
+U8 = mybir.dt.uint8
+FP8X4 = mybir.dt.float8_e4m3fn_x4
+FP4X4 = mybir.dt.float4_e2m1fn_x4
+COPY = mybir.ActivationFunctionType.Copy
+RELU = mybir.ActivationFunctionType.Relu
+
+P = 128
+PACK = 4
+NODE_CHUNKS = (512, 512, 512, 256, 256)
+EDGE_CHUNK = 128
+W_HALF = H // 2
+LINE = 4
+
+
+def tile_picked_edgeup_relu_e_kernel(tc, xT, eT, w1, w2, w3, w4_words, w4_scales, offs, out):
+    nc = tc.nc
+
+    def cast(on_scalar, dst, src):
+        if on_scalar:
+            nc.scalar.activation(dst, src, COPY)
+        else:
+            nc.vector.tensor_copy(dst, src)
+
+    def interleave(on_scalar, grouped, raw, c0, c1):
+        cast(
+            on_scalar,
+            grouped[:, c0:c1, :].rearrange("p (c i) j -> p c j i", i=LINE),
+            raw[:, :, c0:c1].rearrange("p j (c i) -> p c j i", i=LINE),
+        )
+
+    def quantize(words, scales, values):
+        nc.vector.quantize_mx(out=words.bitcast(FP8X4), scales=scales, in_=values)
+
+    with ExitStack() as ctx:
+        keep = ctx.enter_context(tc.tile_pool(name="keep", bufs=1))
+        psum = ctx.enter_context(tc.psum_pool(name="psum", bufs=1))
+
+        offsets = keep.tile([P, S // 16], U16, name="offsets")
+        nc.sync.dma_start(offsets[:], offs)
+
+        x_rows = xT.rearrange("(p j) c -> p j c", j=PACK)
+        x_raw = []
+        node_cols = [slice(sum(NODE_CHUNKS[:n]), sum(NODE_CHUNKS[: n + 1])) for n in range(len(NODE_CHUNKS))]
+        for n, width in enumerate(NODE_CHUNKS):
+            raw = keep.tile([P, PACK, width], F32, name=f"x_raw{n}")
+            nc.sync.dma_start(raw[:], x_rows[:, :, node_cols[n]])
+            x_raw.append(raw)
+        w_raw = []
+        for i, w in enumerate((w1, w2, w3)):
+            w_rows = w.rearrange("(p j) c -> p j c", j=PACK)
+            halves = []
+            for a in range(2):
+                raw = keep.tile([P, PACK, W_HALF], F32, name=f"w_raw{i}_{a}")
+                nc.sync.dma_start(raw[:], w_rows[:, :, a * W_HALF : (a + 1) * W_HALF])
+                halves.append(raw)
+            w_raw.append(halves)
+        e_rows = eT.rearrange("(p j) c -> p j c", j=PACK)
+        e_raw = []
+        for c in range(V // EDGE_CHUNK):
+            raw = keep.tile([P, PACK, EDGE_CHUNK], F32, name=f"e_raw{c}")
+            nc.sync.dma_start(raw[:], e_rows[:, :, c * EDGE_CHUNK : (c + 1) * EDGE_CHUNK])
+            e_raw.append(raw)
+
+        w4_codes = keep.tile([P, 2 * N], U8, name="w4_codes", align_bytes=64)
+        w4_plane = keep.tile([P, N], U8, name="w4_plane", align_bytes=64)
+        nc.vector.memset(w4_plane[:].bitcast(I32), 0)
+        nc.scalar.dma_start(w4_codes[:].bitcast(I32), w4_words[0].bitcast(I32))
+        for q in range(4):
+            nc.scalar.dma_start(w4_plane[32 * q : 32 * q + 4, :].bitcast(I32), w4_scales[0, 4 * q : 4 * q + 4, :].bitcast(I32))
+
+        x_words = keep.tile([P, T], U32, name="x_words", align_bytes=64)
+        x_scales = keep.tile([P, T], U8, name="x_scales", align_bytes=64)
+        nc.vector.memset(x_scales[:].bitcast(I32), 0)
+        for n, width in enumerate(NODE_CHUNKS):
+            scalar_cols = 3 * width // 8
+            grouped = keep.tile([P, width, PACK], BF16, name=f"x_grouped{n}", align_bytes=64)
+            interleave(True, grouped, x_raw[n], 0, scalar_cols)
+            interleave(False, grouped, x_raw[n], scalar_cols, width)
+            cols = node_cols[n]
+            quantize(x_words[:, cols], x_scales[:, cols], grouped[:].rearrange("p c j -> p (c j)"))
+
+        def gather(side):
+            words = keep.tile([P, V], U32, name=f"end_words{side}", align_bytes=64, tag=f"after_w{side}")
+            scales = keep.tile([P, V], U8, name=f"end_scales{side}", align_bytes=64)
+            picks = offsets[:, side * (V // 16) : (side + 1) * (V // 16)]
+            nc.vector.tensor_copy(words[:], x_words[:].indirect(picks))
+            nc.vector.tensor_copy(scales[:], x_scales[:].indirect(picks))
+            return words, scales
+
+        def deal_weights(i, shares):
+            grouped = keep.tile([P, PACK, P, PACK], BF16, name=f"w_grouped{i}", align_bytes=64, tag=f"after_w{i + 1}")
+            for on_scalar, m0, m1 in shares:
+                a, first = divmod(m0, P // 2)
+                cast(
+                    on_scalar,
+                    grouped[:, :, m0:m1, :].rearrange("p t m j -> p m j t"),
+                    w_raw[i][a][:].rearrange("p j (m t) -> p m j t", t=PACK)[:, first : first + m1 - m0, :, :],
+                )
+            words = keep.tile([P, H], U32, name=f"w_words{i}", align_bytes=64)
+            scales = keep.tile([P, H], U8, name=f"w_scales{i}", align_bytes=64)
+            quantize(words[:], scales[:], grouped[:].rearrange("p t m j -> p (t m j)"))
+            return words, scales
+
+        h_banks = [psum.tile([P, PACK, EDGE_CHUNK], F32, name=f"h_bank{c}") for c in range(V // EDGE_CHUNK)]
+
+        def first_layer_pass(c, weights, moving, cols, opens, closes):
+            for t in range(PACK):
+                nc.tensor.matmul_mx(
+                    out=h_banks[c][:, t, :],
+                    lhsT=weights[0][:, t * P : (t + 1) * P].bitcast(FP8X4),
+                    lhsT_scale=weights[1][:, t * P : (t + 1) * P],
+                    rhs=moving[0][:, cols].bitcast(FP8X4),
+                    rhs_scale=moving[1][:, cols],
+                    start=opens and t == 0,
+                    stop=closes and t == PACK - 1,
+                )
+
+        chunks = range(V // EDGE_CHUNK)
+        sources = gather(0)
+        w1_mx = deal_weights(0, [(True, 0, 64), (True, 64, 128)])
+        for c in chunks:
+            first_layer_pass(c, w1_mx, sources, slice(c * EDGE_CHUNK, (c + 1) * EDGE_CHUNK), True, False)
+        destinations = gather(1)
+        w2_mx = deal_weights(1, [(True, 0, 64), (True, 64, 128)])
+        for c in chunks:
+            first_layer_pass(c, w2_mx, destinations, slice(c * EDGE_CHUNK, (c + 1) * EDGE_CHUNK), False, False)
+        w3_mx = deal_weights(2, [(True, 0, 64), (True, 64, 88), (False, 88, 128)])
+
+        out_rows = out.rearrange("(a p) v -> p a v", p=P)
+
+        def edge_features(c, on_scalar):
+            grouped = keep.tile([P, EDGE_CHUNK, PACK], BF16, name=f"e_grouped{c}", align_bytes=64)
+            interleave(on_scalar, grouped, e_raw[c], 0, EDGE_CHUNK)
+            words = keep.tile([P, EDGE_CHUNK], U32, name=f"e_words{c}", align_bytes=64)
+            scales = keep.tile([P, EDGE_CHUNK], U8, name=f"e_scales{c}", align_bytes=64)
+            quantize(words[:], scales[:], grouped[:].rearrange("p c j -> p (c j)"))
+            first_layer_pass(c, w3_mx, (words, scales), slice(0, EDGE_CHUNK), False, True)
+
+        def second_layer(c, on_scalar):
+            h = keep.tile([P, EDGE_CHUNK, PACK], BF16, name=f"h{c}", align_bytes=64)
+            if c < 3:
+                nc.scalar.activation(h[:], h_banks[c][:].rearrange("p t v -> p v t"), RELU)
+            else:
+                nc.vector.tensor_scalar_max(h[:], h_banks[c][:].rearrange("p t v -> p v t"), 0.0)
+            words = keep.tile([P, EDGE_CHUNK], U32, name=f"h_words{c}", align_bytes=64)
+            scales = keep.tile([P, EDGE_CHUNK], U8, name=f"h_scales{c}", align_bytes=64)
+            quantize(words[:], scales[:], h[:].rearrange("p v t -> p (v t)"))
+            bank = psum.tile([P, N // P, EDGE_CHUNK], F32, name=f"out_bank{c}")
+            for a in range(N // P):
+                nc.tensor.matmul_mx(
+                    out=bank[:, a, :],
+                    lhsT=w4_codes[:, 2 * a * P : 2 * (a + 1) * P].bitcast(FP4X4),
+                    lhsT_scale=w4_plane[:, a * P : (a + 1) * P],
+                    rhs=words[:].bitcast(FP8X4),
+                    rhs_scale=scales[:],
+                    start=True,
+                    stop=True,
+                )
+            result = keep.tile([P, N // P, EDGE_CHUNK], F32, name=f"result{c}")
+            cast(on_scalar, result[:], bank[:])
+            nc.sync.dma_start(out_rows[:, :, c * EDGE_CHUNK : (c + 1) * EDGE_CHUNK], result[:])
+
+        for c in chunks:
+            edge_features(c, c == 0)
+        for c in chunks:
+            second_layer(c, c in (1, 2))

@@ -20,8 +20,8 @@ P = 128
 PACK = 4
 NODE_CHUNKS = (512, 512, 512, 256, 256)
 EDGE_CHUNK = 128
-W_HALF = H // 2
 LINE = 4
+STORES = ((0, 2), (0, 2), (2, 1), (3, 1))
 
 
 def tile_picked_edgeup_relu_e_kernel(tc, xT, eT, w1, w2, w3, w4_words, w4_scales, offs, out):
@@ -33,11 +33,11 @@ def tile_picked_edgeup_relu_e_kernel(tc, xT, eT, w1, w2, w3, w4_words, w4_scales
         else:
             nc.vector.tensor_copy(dst, src)
 
-    def interleave(on_scalar, grouped, raw, c0, c1):
+    def interleave(on_scalar, grouped, raw):
         cast(
             on_scalar,
-            grouped[:, c0:c1, :].rearrange("p (c i) j -> p c j i", i=LINE),
-            raw[:, :, c0:c1].rearrange("p j (c i) -> p c j i", i=LINE),
+            grouped.rearrange("p (c i) j -> p c j i", i=LINE),
+            raw.rearrange("p j (c i) -> p c j i", i=LINE),
         )
 
     def quantize(words, scales, values):
@@ -59,58 +59,63 @@ def tile_picked_edgeup_relu_e_kernel(tc, xT, eT, w1, w2, w3, w4_words, w4_scales
             x_raw.append(raw)
         w_raw = []
         for i, w in enumerate((w1, w2, w3)):
-            w_rows = w.rearrange("(p j) c -> p j c", j=PACK)
-            halves = []
-            for a in range(2):
-                raw = keep.tile([P, PACK, W_HALF], F32, name=f"w_raw{i}_{a}")
-                nc.sync.dma_start(raw[:], w_rows[:, :, a * W_HALF : (a + 1) * W_HALF])
-                halves.append(raw)
-            w_raw.append(halves)
+            raw = keep.tile([P, PACK, H], F32, name=f"w_raw{i}")
+            nc.sync.dma_start(raw[:], w.rearrange("(p j) c -> p j c", j=PACK))
+            w_raw.append(raw)
         e_rows = eT.rearrange("(p j) c -> p j c", j=PACK)
         e_raw = []
-        for c in range(V // EDGE_CHUNK):
-            raw = keep.tile([P, PACK, EDGE_CHUNK], F32, name=f"e_raw{c}")
-            nc.sync.dma_start(raw[:], e_rows[:, :, c * EDGE_CHUNK : (c + 1) * EDGE_CHUNK])
+        for a in range(2):
+            raw = keep.tile([P, PACK, V // 2], F32, name=f"e_raw{a}")
+            nc.sync.dma_start(raw[:], e_rows[:, :, a * (V // 2) : (a + 1) * (V // 2)])
             e_raw.append(raw)
 
         w4_codes = keep.tile([P, 2 * N], U8, name="w4_codes", align_bytes=64)
         w4_plane = keep.tile([P, N], U8, name="w4_plane", align_bytes=64)
-        nc.vector.memset(w4_plane[:].bitcast(I32), 0)
-        nc.scalar.dma_start(w4_codes[:].bitcast(I32), w4_words[0].bitcast(I32))
+        nc.gpsimd.memset(w4_plane[:].bitcast(I32), 0)
+        nc.gpsimd.dma_start(w4_codes[:].bitcast(I32), w4_words[0].bitcast(I32))
         for q in range(4):
-            nc.scalar.dma_start(w4_plane[32 * q : 32 * q + 4, :].bitcast(I32), w4_scales[0, 4 * q : 4 * q + 4, :].bitcast(I32))
+            nc.gpsimd.dma_start(w4_plane[32 * q : 32 * q + 4, :].bitcast(I32), w4_scales[0, 4 * q : 4 * q + 4, :].bitcast(I32))
 
         x_words = keep.tile([P, T], U32, name="x_words", align_bytes=64)
         x_scales = keep.tile([P, T], U8, name="x_scales", align_bytes=64)
         nc.vector.memset(x_scales[:].bitcast(I32), 0)
         for n, width in enumerate(NODE_CHUNKS):
-            scalar_cols = 3 * width // 8
-            grouped = keep.tile([P, width, PACK], BF16, name=f"x_grouped{n}", align_bytes=64)
-            interleave(True, grouped, x_raw[n], 0, scalar_cols)
-            interleave(False, grouped, x_raw[n], scalar_cols, width)
-            cols = node_cols[n]
-            quantize(x_words[:, cols], x_scales[:, cols], grouped[:].rearrange("p c j -> p (c j)"))
+            half = width // 2
+            grouped = [keep.tile([P, half, PACK], BF16, name=f"x_grouped{n}_{a}", align_bytes=64) for a in range(2)]
+            for a in range(2):
+                interleave(a == 1, grouped[a][:], x_raw[n][:, :, a * half : (a + 1) * half])
+            for a in range(2):
+                cols = slice(node_cols[n].start + a * half, node_cols[n].start + (a + 1) * half)
+                quantize(x_words[:, cols], x_scales[:, cols], grouped[a][:].rearrange("p c j -> p (c j)"))
 
         def gather(side):
-            words = keep.tile([P, V], U32, name=f"end_words{side}", align_bytes=64, tag=f"after_w{side}")
-            scales = keep.tile([P, V], U8, name=f"end_scales{side}", align_bytes=64)
+            words = keep.tile([P, V], U32, name=f"end_words{side}", align_bytes=64)
+            scales = keep.tile([P, V], U8, name=f"end_scales{side}", align_bytes=64, tag=f"after_w{side}_0")
             picks = offsets[:, side * (V // 16) : (side + 1) * (V // 16)]
             nc.vector.tensor_copy(words[:], x_words[:].indirect(picks))
             nc.vector.tensor_copy(scales[:], x_scales[:].indirect(picks))
             return words, scales
 
-        def deal_weights(i, shares):
-            grouped = keep.tile([P, PACK, P, PACK], BF16, name=f"w_grouped{i}", align_bytes=64, tag=f"after_w{i + 1}")
-            for on_scalar, m0, m1 in shares:
-                a, first = divmod(m0, P // 2)
+        def deal_weights(i, engines):
+            words = keep.tile([P, PACK, P], U32, name=f"w_words{i}", align_bytes=64)
+            scales = keep.tile([P, PACK, P], U8, name=f"w_scales{i}", align_bytes=64)
+            rows = P // len(engines)
+            grouped = []
+            for a, on_scalar in enumerate(engines):
+                part = keep.tile([P, PACK, rows, PACK], BF16, name=f"w_grouped{i}_{a}", align_bytes=64, tag=f"after_w{i + 1}_{a}")
                 cast(
                     on_scalar,
-                    grouped[:, :, m0:m1, :].rearrange("p t m j -> p m j t"),
-                    w_raw[i][a][:].rearrange("p j (m t) -> p m j t", t=PACK)[:, first : first + m1 - m0, :, :],
+                    part[:].rearrange("p t m j -> p m j t"),
+                    w_raw[i][:].rearrange("p j (m t) -> p m j t", t=PACK)[:, a * rows : (a + 1) * rows, :, :],
                 )
-            words = keep.tile([P, H], U32, name=f"w_words{i}", align_bytes=64)
-            scales = keep.tile([P, H], U8, name=f"w_scales{i}", align_bytes=64)
-            quantize(words[:], scales[:], grouped[:].rearrange("p t m j -> p (t m j)"))
+                grouped.append(part)
+            if len(engines) == 1:
+                quantize(words[:].rearrange("p t m -> p (t m)"), scales[:].rearrange("p t m -> p (t m)"), grouped[0][:].rearrange("p t m j -> p (t m j)"))
+            else:
+                for a, part in enumerate(grouped):
+                    for t in range(PACK):
+                        ms = slice(a * rows, (a + 1) * rows)
+                        quantize(words[:, t, ms], scales[:, t, ms], part[:, t, :, :].rearrange("p m j -> p (m j)"))
             return words, scales
 
         h_banks = [psum.tile([P, PACK, EDGE_CHUNK], F32, name=f"h_bank{c}") for c in range(V // EDGE_CHUNK)]
@@ -119,8 +124,8 @@ def tile_picked_edgeup_relu_e_kernel(tc, xT, eT, w1, w2, w3, w4_words, w4_scales
             for t in range(PACK):
                 nc.tensor.matmul_mx(
                     out=h_banks[c][:, t, :],
-                    lhsT=weights[0][:, t * P : (t + 1) * P].bitcast(FP8X4),
-                    lhsT_scale=weights[1][:, t * P : (t + 1) * P],
+                    lhsT=weights[0][:, t, :].bitcast(FP8X4),
+                    lhsT_scale=weights[1][:, t, :],
                     rhs=moving[0][:, cols].bitcast(FP8X4),
                     rhs_scale=moving[1][:, cols],
                     start=opens and t == 0,
@@ -129,20 +134,20 @@ def tile_picked_edgeup_relu_e_kernel(tc, xT, eT, w1, w2, w3, w4_words, w4_scales
 
         chunks = range(V // EDGE_CHUNK)
         sources = gather(0)
-        w1_mx = deal_weights(0, [(True, 0, 64), (True, 64, 128)])
+        w1_mx = deal_weights(0, [True])
         for c in chunks:
             first_layer_pass(c, w1_mx, sources, slice(c * EDGE_CHUNK, (c + 1) * EDGE_CHUNK), True, False)
         destinations = gather(1)
-        w2_mx = deal_weights(1, [(True, 0, 64), (True, 64, 128)])
+        w2_mx = deal_weights(1, [True])
         for c in chunks:
             first_layer_pass(c, w2_mx, destinations, slice(c * EDGE_CHUNK, (c + 1) * EDGE_CHUNK), False, False)
-        w3_mx = deal_weights(2, [(True, 0, 64), (True, 64, 88), (False, 88, 128)])
+        w3_mx = deal_weights(2, [True, False])
 
         out_rows = out.rearrange("(a p) v -> p a v", p=P)
 
         def edge_features(c, on_scalar):
-            grouped = keep.tile([P, EDGE_CHUNK, PACK], BF16, name=f"e_grouped{c}", align_bytes=64)
-            interleave(on_scalar, grouped, e_raw[c], 0, EDGE_CHUNK)
+            grouped = keep.tile([P, EDGE_CHUNK, PACK], BF16, name=f"e_grouped{c}", align_bytes=64, tag=f"after_e{c}")
+            interleave(on_scalar, grouped[:], e_raw[c // 2][:, :, (c % 2) * EDGE_CHUNK : (c % 2 + 1) * EDGE_CHUNK])
             words = keep.tile([P, EDGE_CHUNK], U32, name=f"e_words{c}", align_bytes=64)
             scales = keep.tile([P, EDGE_CHUNK], U8, name=f"e_scales{c}", align_bytes=64)
             quantize(words[:], scales[:], grouped[:].rearrange("p c j -> p (c j)"))
@@ -150,11 +155,11 @@ def tile_picked_edgeup_relu_e_kernel(tc, xT, eT, w1, w2, w3, w4_words, w4_scales
 
         def second_layer(c, on_scalar):
             h = keep.tile([P, EDGE_CHUNK, PACK], BF16, name=f"h{c}", align_bytes=64)
-            if c < 3:
+            if c != 2:
                 nc.scalar.activation(h[:], h_banks[c][:].rearrange("p t v -> p v t"), RELU)
             else:
                 nc.vector.tensor_scalar_max(h[:], h_banks[c][:].rearrange("p t v -> p v t"), 0.0)
-            words = keep.tile([P, EDGE_CHUNK], U32, name=f"h_words{c}", align_bytes=64)
+            words = keep.tile([P, EDGE_CHUNK], U32, name=f"h_words{c}", align_bytes=64, tag=f"after_e{3 - c}")
             scales = keep.tile([P, EDGE_CHUNK], U8, name=f"h_scales{c}", align_bytes=64)
             quantize(words[:], scales[:], h[:].rearrange("p v t -> p (v t)"))
             bank = psum.tile([P, N // P, EDGE_CHUNK], F32, name=f"out_bank{c}")
@@ -168,11 +173,14 @@ def tile_picked_edgeup_relu_e_kernel(tc, xT, eT, w1, w2, w3, w4_words, w4_scales
                     start=True,
                     stop=True,
                 )
-            result = keep.tile([P, N // P, EDGE_CHUNK], F32, name=f"result{c}")
-            cast(on_scalar, result[:], bank[:])
-            nc.sync.dma_start(out_rows[:, :, c * EDGE_CHUNK : (c + 1) * EDGE_CHUNK], result[:])
+            first, count = STORES[c]
+            cols = slice((c - first) * EDGE_CHUNK, (c - first + 1) * EDGE_CHUNK)
+            cast(on_scalar, results[first][:, :, cols], bank[:])
+            if c == first + count - 1:
+                nc.sync.dma_start(out_rows[:, :, first * EDGE_CHUNK : (c + 1) * EDGE_CHUNK], results[first][:])
 
+        results = {first: keep.tile([P, N // P, count * EDGE_CHUNK], F32, name=f"result{first}") for first, count in sorted(set(STORES))}
         for c in chunks:
-            edge_features(c, c == 0)
+            edge_features(c, c % 2 == 0)
         for c in chunks:
-            second_layer(c, c in (1, 2))
+            second_layer(c, c != 2)

@@ -48,7 +48,6 @@ def tile_picked_edgeup_relu_e_kernel(tc, xT, eT, w1, w2, w3, w4_words, w4_scales
         psum = ctx.enter_context(tc.psum_pool(name="psum", bufs=1))
 
         offsets = keep.tile([P, S // 16], U16, name="offsets")
-        nc.sync.dma_start(offsets[:], offs)
 
         x_rows = xT.rearrange("(p j) c -> p j c", j=PACK)
         x_raw = []
@@ -57,16 +56,21 @@ def tile_picked_edgeup_relu_e_kernel(tc, xT, eT, w1, w2, w3, w4_words, w4_scales
             raw = keep.tile([P, PACK, width], F32, name=f"x_raw{n}")
             nc.sync.dma_start(raw[:], x_rows[:, :, node_cols[n]])
             x_raw.append(raw)
+        nc.sync.dma_start(offsets[:], offs)
         w_raw = []
         for i, w in enumerate((w1, w2, w3)):
-            raw = keep.tile([P, PACK, H], F32, name=f"w_raw{i}")
-            nc.sync.dma_start(raw[:], w.rearrange("(p j) c -> p j c", j=PACK))
-            w_raw.append(raw)
+            w_rows = w.rearrange("(p j) c -> p j c", j=PACK)
+            halves = []
+            for a in range(2):
+                raw = keep.tile([P, PACK, H // 2], F32, name=f"w_raw{i}_{a}")
+                nc.sync.dma_start(raw[:], w_rows[:, :, a * (H // 2) : (a + 1) * (H // 2)])
+                halves.append(raw)
+            w_raw.append(halves)
         e_rows = eT.rearrange("(p j) c -> p j c", j=PACK)
         e_raw = []
-        for a in range(2):
-            raw = keep.tile([P, PACK, V // 2], F32, name=f"e_raw{a}")
-            nc.sync.dma_start(raw[:], e_rows[:, :, a * (V // 2) : (a + 1) * (V // 2)])
+        for c in range(V // EDGE_CHUNK):
+            raw = keep.tile([P, PACK, EDGE_CHUNK], F32, name=f"e_raw{c}")
+            nc.sync.dma_start(raw[:], e_rows[:, :, c * EDGE_CHUNK : (c + 1) * EDGE_CHUNK])
             e_raw.append(raw)
 
         w4_codes = keep.tile([P, 2 * N], U8, name="w4_codes", align_bytes=64)
@@ -90,32 +94,33 @@ def tile_picked_edgeup_relu_e_kernel(tc, xT, eT, w1, w2, w3, w4_words, w4_scales
 
         def gather(side):
             words = keep.tile([P, V], U32, name=f"end_words{side}", align_bytes=64)
-            scales = keep.tile([P, V], U8, name=f"end_scales{side}", align_bytes=64, tag=f"after_w{side}_0")
+            scales = keep.tile([P, V], U8, name=f"end_scales{side}", align_bytes=64, tag=f"after_w{side}")
             picks = offsets[:, side * (V // 16) : (side + 1) * (V // 16)]
             nc.vector.tensor_copy(words[:], x_words[:].indirect(picks))
             nc.vector.tensor_copy(scales[:], x_scales[:].indirect(picks))
             return words, scales
 
-        def deal_weights(i, engines):
+        half_rows = P // 2
+
+        def deal(on_scalar, grouped, raw):
+            cast(on_scalar, grouped.rearrange("p t m j -> p m j t"), raw.rearrange("p j (m t) -> p m j t", t=PACK))
+
+        def deal_weights(i, shared):
             words = keep.tile([P, PACK, P], U32, name=f"w_words{i}", align_bytes=64)
             scales = keep.tile([P, PACK, P], U8, name=f"w_scales{i}", align_bytes=64)
-            rows = P // len(engines)
-            grouped = []
-            for a, on_scalar in enumerate(engines):
-                part = keep.tile([P, PACK, rows, PACK], BF16, name=f"w_grouped{i}_{a}", align_bytes=64, tag=f"after_w{i + 1}_{a}")
-                cast(
-                    on_scalar,
-                    part[:].rearrange("p t m j -> p m j t"),
-                    w_raw[i][:].rearrange("p j (m t) -> p m j t", t=PACK)[:, a * rows : (a + 1) * rows, :, :],
-                )
-                grouped.append(part)
-            if len(engines) == 1:
-                quantize(words[:].rearrange("p t m -> p (t m)"), scales[:].rearrange("p t m -> p (t m)"), grouped[0][:].rearrange("p t m j -> p (t m j)"))
-            else:
-                for a, part in enumerate(grouped):
+            if shared:
+                parts = [keep.tile([P, PACK, half_rows, PACK], BF16, name=f"w_grouped{i}_{a}", align_bytes=64) for a in range(2)]
+                for a in range(2):
+                    deal(a == 0, parts[a][:], w_raw[i][a][:])
+                for a in range(2):
                     for t in range(PACK):
-                        ms = slice(a * rows, (a + 1) * rows)
-                        quantize(words[:, t, ms], scales[:, t, ms], part[:, t, :, :].rearrange("p m j -> p (m j)"))
+                        ms = slice(a * half_rows, (a + 1) * half_rows)
+                        quantize(words[:, t, ms], scales[:, t, ms], parts[a][:, t, :, :].rearrange("p m j -> p (m j)"))
+            else:
+                grouped = keep.tile([P, PACK, P, PACK], BF16, name=f"w_grouped{i}", align_bytes=64, tag=f"after_w{i + 1}")
+                for a in range(2):
+                    deal(True, grouped[:, :, a * half_rows : (a + 1) * half_rows, :], w_raw[i][a][:])
+                quantize(words[:].rearrange("p t m -> p (t m)"), scales[:].rearrange("p t m -> p (t m)"), grouped[:].rearrange("p t m j -> p (t m j)"))
             return words, scales
 
         h_banks = [psum.tile([P, PACK, EDGE_CHUNK], F32, name=f"h_bank{c}") for c in range(V // EDGE_CHUNK)]
@@ -134,20 +139,20 @@ def tile_picked_edgeup_relu_e_kernel(tc, xT, eT, w1, w2, w3, w4_words, w4_scales
 
         chunks = range(V // EDGE_CHUNK)
         sources = gather(0)
-        w1_mx = deal_weights(0, [True])
+        w1_mx = deal_weights(0, False)
         for c in chunks:
             first_layer_pass(c, w1_mx, sources, slice(c * EDGE_CHUNK, (c + 1) * EDGE_CHUNK), True, False)
         destinations = gather(1)
-        w2_mx = deal_weights(1, [True])
+        w2_mx = deal_weights(1, False)
         for c in chunks:
             first_layer_pass(c, w2_mx, destinations, slice(c * EDGE_CHUNK, (c + 1) * EDGE_CHUNK), False, False)
-        w3_mx = deal_weights(2, [True, False])
+        w3_mx = deal_weights(2, True)
 
         out_rows = out.rearrange("(a p) v -> p a v", p=P)
 
         def edge_features(c, on_scalar):
             grouped = keep.tile([P, EDGE_CHUNK, PACK], BF16, name=f"e_grouped{c}", align_bytes=64, tag=f"after_e{c}")
-            interleave(on_scalar, grouped[:], e_raw[c // 2][:, :, (c % 2) * EDGE_CHUNK : (c % 2 + 1) * EDGE_CHUNK])
+            interleave(on_scalar, grouped[:], e_raw[c][:])
             words = keep.tile([P, EDGE_CHUNK], U32, name=f"e_words{c}", align_bytes=64)
             scales = keep.tile([P, EDGE_CHUNK], U8, name=f"e_scales{c}", align_bytes=64)
             quantize(words[:], scales[:], grouped[:].rearrange("p c j -> p (c j)"))
@@ -155,7 +160,7 @@ def tile_picked_edgeup_relu_e_kernel(tc, xT, eT, w1, w2, w3, w4_words, w4_scales
 
         def second_layer(c, on_scalar):
             h = keep.tile([P, EDGE_CHUNK, PACK], BF16, name=f"h{c}", align_bytes=64)
-            if c != 2:
+            if c != 3:
                 nc.scalar.activation(h[:], h_banks[c][:].rearrange("p t v -> p v t"), RELU)
             else:
                 nc.vector.tensor_scalar_max(h[:], h_banks[c][:].rearrange("p t v -> p v t"), 0.0)
@@ -181,6 +186,6 @@ def tile_picked_edgeup_relu_e_kernel(tc, xT, eT, w1, w2, w3, w4_words, w4_scales
 
         results = {first: keep.tile([P, N // P, count * EDGE_CHUNK], F32, name=f"result{first}") for first, count in sorted(set(STORES))}
         for c in chunks:
-            edge_features(c, c % 2 == 0)
+            edge_features(c, c < 2)
         for c in chunks:
-            second_layer(c, c != 2)
+            second_layer(c, c != 3)

from contextlib import ExitStack

import concourse.mybir as mybir

K, T, S, V, H, N = 512, 2048, 1024, 512, 512, 256
FLOPS = 2 * (3 * K * H * V + H * N * V)

F32 = mybir.dt.float32
BF16 = mybir.dt.bfloat16
I32 = mybir.dt.int32
U32 = mybir.dt.uint32
U16 = mybir.dt.uint16
U8 = mybir.dt.uint8
FP8X4 = mybir.dt.float8_e4m3fn_x4
FP4X4 = mybir.dt.float4_e2m1fn_x4
COPY = mybir.ActivationFunctionType.Copy
RELU = mybir.ActivationFunctionType.Relu

P = 128
PACK = 4
NODE_CHUNKS = (512, 512, 512, 256, 256)
EDGE_CHUNK = 128
LINE = 4
STORES = ((0, 2), (0, 2), (2, 1), (3, 1))


def tile_picked_edgeup_relu_e_kernel(tc, xT, eT, w1, w2, w3, w4_words, w4_scales, offs, out):
    nc = tc.nc

    def cast(on_scalar, dst, src):
        if on_scalar:
            nc.scalar.activation(dst, src, COPY)
        else:
            nc.vector.tensor_copy(dst, src)

    def interleave(on_scalar, grouped, raw):
        cast(
            on_scalar,
            grouped.rearrange("p (c i) j -> p c j i", i=LINE),
            raw.rearrange("p j (c i) -> p c j i", i=LINE),
        )

    def quantize(words, scales, values):
        nc.vector.quantize_mx(out=words.bitcast(FP8X4), scales=scales, in_=values)

    with ExitStack() as ctx:
        keep = ctx.enter_context(tc.tile_pool(name="keep", bufs=1))
        psum = ctx.enter_context(tc.psum_pool(name="psum", bufs=1))

        offsets = keep.tile([P, S // 16], U16, name="offsets")

        x_rows = xT.rearrange("(p j) c -> p j c", j=PACK)
        x_raw = []
        node_cols = [slice(sum(NODE_CHUNKS[:n]), sum(NODE_CHUNKS[: n + 1])) for n in range(len(NODE_CHUNKS))]
        for n, width in enumerate(NODE_CHUNKS):
            raw = keep.tile([P, PACK, width], F32, name=f"x_raw{n}")
            nc.sync.dma_start(raw[:], x_rows[:, :, node_cols[n]])
            x_raw.append(raw)
        nc.sync.dma_start(offsets[:], offs)
        w_raw = []
        for i, w in enumerate((w1, w2, w3)):
            w_rows = w.rearrange("(p j) c -> p j c", j=PACK)
            halves = []
            for a in range(2):
                raw = keep.tile([P, PACK, H // 2], F32, name=f"w_raw{i}_{a}")
                nc.sync.dma_start(raw[:], w_rows[:, :, a * (H // 2) : (a + 1) * (H // 2)])
                halves.append(raw)
            w_raw.append(halves)
        e_rows = eT.rearrange("(p j) c -> p j c", j=PACK)
        e_raw = []
        for c in range(V // EDGE_CHUNK):
            raw = keep.tile([P, PACK, EDGE_CHUNK], F32, name=f"e_raw{c}")
            nc.sync.dma_start(raw[:], e_rows[:, :, c * EDGE_CHUNK : (c + 1) * EDGE_CHUNK])
            e_raw.append(raw)

        w4_codes = keep.tile([P, 2 * N], U8, name="w4_codes", align_bytes=64)
        w4_plane = keep.tile([P, N], U8, name="w4_plane", align_bytes=64)
        nc.gpsimd.memset(w4_plane[:].bitcast(I32), 0)
        nc.gpsimd.dma_start(w4_codes[:].bitcast(I32), w4_words[0].bitcast(I32))
        for q in range(4):
            nc.gpsimd.dma_start(w4_plane[32 * q : 32 * q + 4, :].bitcast(I32), w4_scales[0, 4 * q : 4 * q + 4, :].bitcast(I32))

        x_words = keep.tile([P, T], U32, name="x_words", align_bytes=64)
        x_scales = keep.tile([P, T], U8, name="x_scales", align_bytes=64)
        nc.vector.memset(x_scales[:].bitcast(I32), 0)
        for n, width in enumerate(NODE_CHUNKS):
            half = width // 2
            grouped = [keep.tile([P, half, PACK], BF16, name=f"x_grouped{n}_{a}", align_bytes=64) for a in range(2)]
            for a in range(2):
                interleave(a == 1, grouped[a][:], x_raw[n][:, :, a * half : (a + 1) * half])
            for a in range(2):
                cols = slice(node_cols[n].start + a * half, node_cols[n].start + (a + 1) * half)
                quantize(x_words[:, cols], x_scales[:, cols], grouped[a][:].rearrange("p c j -> p (c j)"))

        def gather(side):
            words = keep.tile([P, V], U32, name=f"end_words{side}", align_bytes=64)
            scales = keep.tile([P, V], U8, name=f"end_scales{side}", align_bytes=64, tag=f"after_w{side}")
            picks = offsets[:, side * (V // 16) : (side + 1) * (V // 16)]
            nc.vector.tensor_copy(words[:], x_words[:].indirect(picks))
            nc.vector.tensor_copy(scales[:], x_scales[:].indirect(picks))
            return words, scales

        half_rows = P // 2

        def deal(on_scalar, grouped, raw):
            cast(on_scalar, grouped.rearrange("p t m j -> p m j t"), raw.rearrange("p j (m t) -> p m j t", t=PACK))

        def deal_weights(i, shared):
            words = keep.tile([P, PACK, P], U32, name=f"w_words{i}", align_bytes=64)
            scales = keep.tile([P, PACK, P], U8, name=f"w_scales{i}", align_bytes=64)
            if shared:
                parts = [keep.tile([P, PACK, half_rows, PACK], BF16, name=f"w_grouped{i}_{a}", align_bytes=64) for a in range(2)]
                for a in range(2):
                    deal(a == 0, parts[a][:], w_raw[i][a][:])
                for a in range(2):
                    for t in range(PACK):
                        ms = slice(a * half_rows, (a + 1) * half_rows)
                        quantize(words[:, t, ms], scales[:, t, ms], parts[a][:, t, :, :].rearrange("p m j -> p (m j)"))
            else:
                grouped = keep.tile([P, PACK, P, PACK], BF16, name=f"w_grouped{i}", align_bytes=64, tag=f"after_w{i + 1}")
                for a in range(2):
                    deal(True, grouped[:, :, a * half_rows : (a + 1) * half_rows, :], w_raw[i][a][:])
                quantize(words[:].rearrange("p t m -> p (t m)"), scales[:].rearrange("p t m -> p (t m)"), grouped[:].rearrange("p t m j -> p (t m j)"))
            return words, scales

        h_banks = [psum.tile([P, PACK, EDGE_CHUNK], F32, name=f"h_bank{c}") for c in range(V // EDGE_CHUNK)]

        def first_layer_pass(c, weights, moving, cols, opens, closes):
            for t in range(PACK):
                nc.tensor.matmul_mx(
                    out=h_banks[c][:, t, :],
                    lhsT=weights[0][:, t, :].bitcast(FP8X4),
                    lhsT_scale=weights[1][:, t, :],
                    rhs=moving[0][:, cols].bitcast(FP8X4),
                    rhs_scale=moving[1][:, cols],
                    start=opens and t == 0,
                    stop=closes and t == PACK - 1,
                )

        chunks = range(V // EDGE_CHUNK)
        sources = gather(0)
        w1_mx = deal_weights(0, False)
        for c in chunks:
            first_layer_pass(c, w1_mx, sources, slice(c * EDGE_CHUNK, (c + 1) * EDGE_CHUNK), True, False)
        destinations = gather(1)
        w2_mx = deal_weights(1, False)
        for c in chunks:
            first_layer_pass(c, w2_mx, destinations, slice(c * EDGE_CHUNK, (c + 1) * EDGE_CHUNK), False, False)
        w3_mx = deal_weights(2, True)

        out_rows = out.rearrange("(a p) v -> p a v", p=P)

        def edge_features(c, on_scalar):
            grouped = keep.tile([P, EDGE_CHUNK, PACK], BF16, name=f"e_grouped{c}", align_bytes=64, tag=f"after_e{c}")
            interleave(on_scalar, grouped[:], e_raw[c][:])
            words = keep.tile([P, EDGE_CHUNK], U32, name=f"e_words{c}", align_bytes=64)
            scales = keep.tile([P, EDGE_CHUNK], U8, name=f"e_scales{c}", align_bytes=64)
            quantize(words[:], scales[:], grouped[:].rearrange("p c j -> p (c j)"))
            first_layer_pass(c, w3_mx, (words, scales), slice(0, EDGE_CHUNK), False, True)

        def second_layer(c, on_scalar):
            h = keep.tile([P, EDGE_CHUNK, PACK], BF16, name=f"h{c}", align_bytes=64)
            if c != 3:
                nc.scalar.activation(h[:], h_banks[c][:].rearrange("p t v -> p v t"), RELU)
            else:
                nc.vector.tensor_scalar_max(h[:], h_banks[c][:].rearrange("p t v -> p v t"), 0.0)
            words = keep.tile([P, EDGE_CHUNK], U32, name=f"h_words{c}", align_bytes=64, tag=f"after_e{3 - c}")
            scales = keep.tile([P, EDGE_CHUNK], U8, name=f"h_scales{c}", align_bytes=64)
            quantize(words[:], scales[:], h[:].rearrange("p v t -> p (v t)"))
            bank = psum.tile([P, N // P, EDGE_CHUNK], F32, name=f"out_bank{c}")
            for a in range(N // P):
                nc.tensor.matmul_mx(
                    out=bank[:, a, :],
                    lhsT=w4_codes[:, 2 * a * P : 2 * (a + 1) * P].bitcast(FP4X4),
                    lhsT_scale=w4_plane[:, a * P : (a + 1) * P],
                    rhs=words[:].bitcast(FP8X4),
                    rhs_scale=scales[:],
                    start=True,
                    stop=True,
                )
            first, count = STORES[c]
            cols = slice((c - first) * EDGE_CHUNK, (c - first + 1) * EDGE_CHUNK)
            cast(on_scalar, results[first][:, :, cols], bank[:])
            if c == first + count - 1:
                nc.sync.dma_start(out_rows[:, :, first * EDGE_CHUNK : (c + 1) * EDGE_CHUNK], results[first][:])

        results = {first: keep.tile([P, N // P, count * EDGE_CHUNK], F32, name=f"result{first}") for first, count in sorted(set(STORES))}
        for c in chunks:
            edge_features(c, c < 2)
        for c in chunks:
            second_layer(c, c != 3)
